import numpy as np, ml_dtypes
CORES = [40,41,42,43,44,45,46,47]
N = 8
import mx_ref
BF = ml_dtypes.bfloat16
def gentries(a):
    return np.ascontiguousarray(a.reshape(8, 16, -1).transpose(0, 2, 1)).reshape(8, -1)
def gtable(e):
    e = np.asarray(e); return np.ascontiguousarray(e.reshape(8, -1, 16).transpose(0, 2, 1)).reshape(128, -1).astype(np.int32)
def gcols(t, e):
    v = np.concatenate([t.reshape(8, 16, -1, 4), np.zeros((8, 16, 1, 4), BF)], axis=2)
    return np.ascontiguousarray(np.stack([v[g][:, e[g]] for g in range(8)])).reshape(128, -1)
def tile(rs):
    return np.stack(rs, axis=2).reshape(128, -1).astype(BF)
def pick(q, e):
    c = np.concatenate([q[0].reshape(128, -1, 4), np.zeros((128, 1, 4), np.uint8)], axis=1); s = np.concatenate([q[1], np.ones((16, 1), np.uint8)], axis=1)
    return (np.ascontiguousarray(c[:, e].reshape(128, -1)), np.ascontiguousarray(s[:, e]))
def join(*qs):
    return (np.concatenate([q[0] for q in qs], axis=1), np.concatenate([q[1] for q in qs], axis=1))
def put(q, e, v):
    c, s = q[0].reshape(128, -1, 4).copy(), q[1].copy(); c[:, e] = v[0].reshape(128, -1, 4); s[:, e] = v[1]
    return (c.reshape(128, -1), s)
def pk(c, s):
    return (np.ascontiguousarray(c), mx_ref.live(s))
def emit(q):
    return q[0], q[1]
def packed(v, rng):
    q = [mx_ref.quantize(np.ascontiguousarray(v[r])) for r in range(N)]
    return np.stack([a for a, b in q]), np.stack([mx_ref.plane(b, rng) for a, b in q])
def values_of_codes():
    e, c = np.zeros((128, 128, 4), np.float32), np.zeros((128, 2, 4), np.uint8)
    e[np.arange(128), np.arange(128), 0] = 1
    c[:127, :, 0] = np.arange(256).reshape(2, 128).T[:127]
    return mx_ref.matmul(mx_ref.quantize(e.reshape(128, 512).astype(BF)), (c.reshape(128, 8), np.full((16, 2), 127, np.uint8))).T.reshape(-1).astype(np.float64)
CODE_VALUE, SCALE_VALUE = values_of_codes(), 2.0 ** (np.arange(256) - 127.0)
def decode(q):
    return (CODE_VALUE[q[0]].reshape(16, 8, -1, 4) * SCALE_VALUE[q[1]][:, None, :, None] + 0.0).reshape(128, -1).astype(np.float32)
def f(rng, *shape):
    return mx_ref.flush((rng.standard_normal(shape, dtype=np.float32) * np.exp2(rng.integers(-2, 3, shape[:-1] + (1,)))).astype(BF))
def wide(rng, *shape, cols=0):
    v = rng.standard_normal(shape, dtype=np.float32) * np.exp2(rng.integers(-12, 13, shape)).astype(np.float32)
    if cols: v *= np.repeat(np.exp2(rng.integers(-cols, cols + 1, shape[:-2] + (1, shape[-1] // 4))) * (rng.random(shape[:-2] + (1, shape[-1] // 4)) > 0.0625), 4, axis=-1).astype(np.float32)
    return mx_ref.flush(v.astype(BF))
C, H = 384, 192
STEP = [1, 2, 4]
PLACES = np.arange(C)
def numbers_of(rng):
    return {"x": np.array(f(rng, N, 128, 4 * C)), "u": np.array(f(rng, N, 128, 512)), "v": np.array(f(rng, N, 128, 512))}
def drawn(rng):
    o = rng.permuted(np.tile(PLACES, (N, 8, 3, 1)), axis=3)
    k = np.zeros_like(o)
    np.put_along_axis(k, o, o.reshape(N, 8, 3, H, 2)[..., ::-1].reshape(N, 8, 3, C), axis=3)
    e = np.tile(PLACES, (N, 8, 1))
    return rng.permuted(e, axis=2), rng.permuted(e, axis=2), k
def stored(p, e, k):
    return {"pp": np.stack([gtable(p[r]) for r in range(N)]), "rf": np.stack([gtable(e[r]) for r in range(N)]), "pr": np.stack([gtable(k[r].reshape(8, 3 * C)) for r in range(N)])}
def layers(rng, still=[]):
    w = np.array(f(rng, N, 128, 2048)).reshape(N, 8, 16, 4, 8, 16, 4)
    for i in still:
        w[:, :, i] = 0
        w[:, :, :, :, :, i] = 0
    return w
def weights(rng, w):
    c, s = packed(np.ascontiguousarray(w).reshape(N, 128, 2048), rng)
    return {"wc": c, "ws": s}
def scoring(d):
    u = d["u"].reshape(N, 128, 128, 4)
    u[:, :, ::16] = 0
    u[:, :, 1::16] = 0
    return u
def setup_inputs(rng):
    return {**numbers_of(rng), **stored(*drawn(rng)), **weights(rng, layers(rng))}
def setup_inputs_ties(rng):
    d = numbers_of(rng)
    p, e, k = drawn(rng)
    o = rng.permutation(N)
    k[o[3], :4] = k[o[3], :4, :1]
    a, b = rng.integers(-1, 2, (2, N, 8, C))
    a[o[0]] = 0
    a[o[1]] = 1
    b[o[1], :4] = 1
    b[o[1], 4:] = 0
    for g in range(4): a[o[3], g, p[o[3], g]] = np.where(PLACES < k[o[3], g, 0], 1, -rng.integers(0, 2, C))
    x = d["x"].reshape(N, 8, 16, C, 4)
    x[:, :, 0] = 0
    x[:, :, 0, :, 0] = a.astype(np.float32).astype(BF)
    x[:, :, 0, :, 1] = b.astype(np.float32).astype(BF)
    u = scoring(d)
    for h in range(0, 128, 16):
        u[:, h, h, 0] = 1
        u[:, h, h + 1, 1] = 1
    return {"x": x.reshape(N, 128, 4 * C), "u": u.reshape(N, 128, 512), "v": d["v"], **stored(p, rng.integers(0, C, (N, 8, C)), k), **weights(rng, layers(rng, [0]))}
def setup_inputs_near(rng):
    d = numbers_of(rng)
    o = rng.permutation(N)
    z = int(np.argmax(o))
    k = np.where(o % 2 == 0, 2.0 ** -30, 1.0)
    x = np.zeros((N, 8, 16, C, 4))
    for i in (0, 2):
        s = rng.integers(-1, 2, (N, 8, C)) * k[:, None, None]
        x[:, :, i, :, 0] = 1.125 * s
        x[:, :, i + 1, :, 0] = -1.25 * s
    for r in range(N):
        at_ = [0, C - 1, int(rng.integers(C)), int(rng.integers(C))]
        for g, j in zip(rng.permutation(8)[:4], at_): x[r, g, 0, j, 0] = 2.0 ** 30 * rng.choice([-1.0, 1.0])
    x[:, :, 8:] = rng.choice([-1.0, 1.0], (N, 8, 8, C, 4)) * (1 + 0.125 * rng.integers(0, 8, (N, 8, 8, C, 4))) * 2.0 ** -30
    x[z, :, :8] = 0
    x[:, :, 7, :, 0] = 2.0 ** -30
    x[:, :, 8, :, 3] = 2.0 ** -30
    u = scoring(d)
    w = layers(rng)
    w[:, :, :8] = 0
    w[:, :, :, :, :, :9] = 0
    for h in range(0, 128, 16):
        for i in (0, 1):
            u[:, h + 2 * i, h + i, 0] = (1.125 * k).astype(np.float32).astype(BF)
            u[:, h + 2 * i + 1, h + i, 0] = k.astype(np.float32).astype(BF)
            u[z, :, h + i] = 0
            u[z, h + 5 + i, h + i, 0] = 2.0 ** -30
            w[z, h // 16, 8, 0, h // 16, 5 + i, i] = 2.0 ** -8
    return {"x": x.astype(np.float32).reshape(N, 128, 4 * C).astype(BF), "u": u.reshape(N, 128, 512), "v": d["v"], **stored(*drawn(rng)), **weights(rng, w)}
def setup_inputs_odd(rng):
    d = numbers_of(rng)
    x = (2 * rng.integers(0, 8, (N, 16, 8, C, 4)) + 1) * 2.0 ** -8 * rng.choice([-1.0, 1.0], (N, 16, 8, C, 4))
    x[:, :, 0, :, 0] = 2.0 ** 8 * np.where(rng.random((N, 16, C)) < 0.5, 1.96875, 1.875)
    u = scoring(d)
    for i in (0, 1):
        x[:, ::2, 1 + 2 * i, :, 0] = (8 + rng.integers(0, 2, (N, 8, C))) * 2.0 ** -8
        x[:, ::2, 2 + 2 * i, :, 0] = 8 * 2.0 ** -8
        for h in range(0, 128, 16):
            u[:, h + 1 + 2 * i, h + i, 0] = 1
            u[:, h + 2 + 2 * i, h + i, 0] = -1
    return {"x": x.astype(np.float32).reshape(N, 128, 4 * C).astype(BF), "u": u.reshape(N, 128, 512), "v": d["v"], **stored(*drawn(rng)), **weights(rng, layers(rng, [0, 1, 2, 3, 4, 8]))}
def setup_inputs_ends(rng):
    d = numbers_of(rng)
    p, q, k = drawn(rng)
    o, e = rng.permutation(N) % 4, rng.permutation(N) % 4
    s = rng.choice([-1.0, 1.0], (N, 128, C, 4))
    s[o == 0] = -1
    s[o == 1] = rng.choice([-1.0, 1.0], (N, 1, C, 1))[o == 1]
    x = s * (0.87 + 0.07 * rng.random((N, 128, C, 4))) * 2.0 ** 30
    x[:, 15::16] = 0
    x[o == 3] = 2.0 ** -30
    size = np.where(o == 3, 2.0 ** -30, 2.0 ** 30)
    u = scoring(d)
    for i in (0, 1):
        a = np.stack([rng.permutation(8) % 2 * 2.0 - 1.0 for r in range(N)]) * size[:, None]
        u[:, :, i::16] = a.astype(np.float32).astype(BF)[:, None, :, None]
    v = rng.choice([-1.0, 1.0], (N, 128, 512)) * np.where(o % 2 == 1, 2.0 ** -30, 2.0 ** 30)[:, None, None]
    p[e == 0] = PLACES
    p[e == 1] = PLACES[::-1]
    q[e == 0] = np.where(np.arange(8) % 2 == 0, C - 1, 0)[:, None]
    q[e == 1] = (rng.integers(0, 2, (N, 8, C)) * (C - 1))[e == 1]
    q[e == 2] = PLACES
    q[e == 3] = rng.integers(0, C, (N, 8, C))[e == 3]
    k[e == 0] = PLACES
    k[e == 1] = PLACES[::-1]
    k[e == 2] = PLACES ^ 1
    w = np.zeros((N, 128, 4, 128, 4), np.float32)
    i = np.arange(128)
    for b in range(4): w[:, i, b, i, b] = np.where(o[:, None] == 3, np.where(i % 16 == 15, 2.0 ** 8, 2.0 ** -8), -0.25)
    return {"x": x.astype(np.float32).reshape(N, 128, 4 * C).astype(BF), "u": u.reshape(N, 128, 512), "v": v.astype(np.float32).astype(BF), **stored(p, q, k), **weights(rng, w.astype(BF))}
def setup_inputs_spread(rng):
    d = setup_inputs(rng)
    d["x"] = wide(rng, N, 128, 4 * C, cols=6)
    return d
def check_inputs(d):
    b = []
    for k in ("x", "u", "v"):
        a = np.abs(d[k].astype(np.float32))
        if not (np.isfinite(a).all() and ((a == 0) | (a >= 2.0 ** -30) & (a <= 2.0 ** 30)).all()): b.append("a value of " + k)
    for k in ("pp", "rf", "pr"):
        if not ((d[k] >= 0) & (d[k] < C)).all(): b.append("an entry of " + k)
    none, least, most = [emit(mx_ref.quantize(np.full((128, 16), k, np.float32).astype(BF)))[1][0, 0] for k in (0.0, 2.0 ** -8, 2.0 ** 8)]
    for r in range(N):
        if not (np.sort(gentries(d["pp"][r]), axis=1) == PLACES).all(): b.append("pp: a column not once in a group")
        k = gentries(d["pr"][r]).reshape(8, 3, C)
        if ((k >= 0) & (k < C)).all() and not (np.take_along_axis(k, k, axis=2) == PLACES).all(): b.append("pr: a place that isn't the pair of its pair")
        if ((d["wc"][r] == 0x7F) | (d["wc"][r] == 0xFF)).any(): b.append("wc: a code that is no number")
        s = mx_ref.live(d["ws"][r])
        if ((s != none) & ((s < least) | (s > most))).any(): b.append("ws: a scale out of range")
        if (((d["wc"][r].reshape(16, 8, 512, 4) & 0x7F) != 0) & (s == none)[:, None, :, None]).any(): b.append("wc: a code other than zero under the scale of zeros")
    return b
def at(a, e):
    return np.take_along_axis(a, e, axis=1)
def layer(w, q):
    return tile([mx_ref.matmul(pick(w, np.arange(128 * b, 128 * b + 128)), q) * np.float32(0.03125) for b in range(4)])
def reference(x, u, v, pp, rf, pr, wc, ws):
    qu = [mx_ref.quantize(u[r]) for r in range(N)]
    lay = [pk(wc[r], ws[r]) for r in range(N)]
    place, refs = [gentries(pp[r]) for r in range(N)], [gentries(rf[r]) for r in range(N)]
    pair = [gentries(pr[r]).reshape(8, 3, C) for r in range(N)]
    now = [x[r] for r in range(N)]
    for t, step in enumerate(STEP):
        held, mix = [], []
        for r in range(N):
            q = mx_ref.quantize(now[r])
            s = mx_ref.matmul(qu[r], q)
            sign, mode = s[::16] > 0, s[1::16] > 0
            held.append(decode(q))
            k, here = pair[r][:, t], at(sign, place[r])
            swap = np.where(here == at(here, k), k, PLACES)
            place[r] = at(place[r], swap)
            old = at(refs[r], swap)
            refs[r] = np.where(at(mode, place[r]), at(swap, old), (old + PLACES - swap) % C)
            g = held[r].astype(BF)
            z = gcols(g, place[r]).astype(np.float32) + gcols(g, at(place[r], refs[r])).astype(np.float32)
            mix.append(mx_ref.quantize((z * np.float32(0.5)).astype(BF)))
        for r in range(N):
            h = layer(lay[r], join(pick(mix[r], np.arange(H)), pick(mix[r ^ step], np.arange(H, C))))
            inverse = np.argsort(place[r], axis=1)
            now[r] = (held[r] + gcols(h, at(refs[r ^ step], at(refs[r], inverse))).astype(np.float32)).astype(BF)
    y, pf = np.zeros((N, 128, C), np.float32), np.zeros((N, 8, 2 * C), np.float32)
    oc, osc = np.zeros((N, 128, 4 * C), np.uint8), np.zeros((N, 16, C), np.uint8)
    for r in range(N):
        q = mx_ref.quantize(now[r])
        y[r] = mx_ref.matmul(mx_ref.quantize(v[r]), q)
        pf[r] = np.concatenate([place[r], refs[r]], axis=1)
        oc[r], osc[r] = emit(q)
    return {"y": y, "pf": pf, "oc": oc, "osc": osc}

@@ -1,0 +1,326 @@
+from concourse.mybir import dt, AluOpType as A, ActivationFunctionType as F
+
+C, H, STEP = 384, 192, [1, 2, 4]
+HOLD = 1408.0
+MID = 192.0
+BF, HF, FL, CODE = "bfloat16", "float16", "float32", "float8_e4m3fn_x4"
+
+SCRATCH = {"ps": ("psum", [128, 4096], "float32")}
+for _n, _c, _d in (
+        [("xin", 1536, BF), ("uin", 512, BF), ("vin", 512, BF), ("ppi", 24, "int32"), ("rfi", 24, "int32"), ("pri", 72, "int32")]
+        + [("wq", 512, CODE), ("wp", 512, "uint8"), ("uq", 128, CODE), ("up", 128, "uint8"), ("uuq", 256, CODE), ("uup", 256, "uint8")]
+        + [("vq", 128, CODE), ("vp", 128, "uint8"), ("eq", 512, CODE), ("ep", 512, "uint8"), ("zlq", H, CODE), ("zlp", H, "uint8")]
+        + [("one", 516, BF), ("eye", 516, BF), ("uoi", 16, "int32"), ("uo", 16, "uint16"), ("cm", C, "int32"), ("pid", 2, "int32")]
+        + [("pmi", 2, "int32"), ("pm", 2, FL), ("cp", 1, FL), ("q16", 24, "int32"), ("qw", 24, FL), ("num", C, FL), ("xd", C, FL)]
+        + [("d1", C, HF), ("d2", C, HF), ("d0", C, HF)]
+        + [(k, 1536, BF) for k in ("fb", "gb", "gc", "bb", "zt", "xt")]
+        + [(k, C, BF) for k in ("aw", "ar", "bw", "br", "pk", "fk", "ir", "ej")]
+        + [(k, C, HF) for k in ("er", "rr", "sc", "sc2", "sc3", "sc4", "scp", "scf")]
+        + [(k, C, FL) for k in ("iv0", "tr", "prow", "frow", "fs", "ef", "yo")]
+        + [(k, 72, FL) for k in ("dcp", "bs", "mu", "sel")]
+        + [(k, 24, FL) for k in ("yy", "y1", "nf", "al", "alc", "mm", "ma", "mx")] + [("pkw", 48, FL), ("ni", 24, "int32")]
+        + [("ku", 72, "uint16"), ("tu", 72, "uint16")] + [(k, 24, "uint16") for k in ("p0", "f0", "iu", "eu", "pku")]
+        + [("xq%d" % t, C, CODE) for t in range(4)] + [("xp%d" % t, C, "uint8") for t in range(4)]
+        + [("%s%d" % (k, t), 72, FL) for k in ("dd", "ba") for t in range(3)]
+        + [("%s%d" % (k, t), 24, "uint16") for k in ("fu", "lf") for t in range(3)]
+        + [("%s%d" % (k, t), H, CODE) for k in ("zuq", "lq") for t in range(3)]
+        + [("%s%d" % (k, t), H, "uint8") for k in ("zup", "lp") for t in range(3)]):
+    SCRATCH[_n] = ("sbuf", [128, _c], _d)
+LOADS = ["x", "u", "v", "pp", "rf", "pr", "wc", "ws"]
+SEMAPHORES = ["qv", "qs", "qt", "qg", "sent", "out"] + ["ld_" + k for k in LOADS] + ["%s%d" % (k, t) for k in ("af", "aq", "ap") for t in range(3)]
+
+
+def rank_program(g, core, T, topo):
+    rank = T.rank_of(core)
+    if rank is None:
+        return
+    queue = {"v": g.vector, "s": g.scalar, "t": g.tensor, "g": g, "y": g.sync}
+    count, know, acc = {}, {k: {} for k in queue}, {}
+
+    def V(name, lo, hi, step=1):
+        return (name, lo, hi, T[name][:, lo:hi] if step == 1 else T[name][:, lo:hi:step])
+
+    def row(name):
+        return V(name, 0, C)
+
+    def bits(v, d=dt.uint8):
+        return (v[0], v[1], v[2], v[3].bitcast(d))
+
+    def ind(win, off):
+        return ("*", win, off, win[3].indirect(off[3]))
+
+    def flat(vs):
+        r = []
+        for v in vs:
+            r += [v[1], v[2]] if v[0] == "*" else [v]
+        return [(n, a, b) if n != "ps" else (n, a // 512 * 512, -(-b // 512) * 512) for n, a, b, _ in r]
+
+    def uses(w, r):
+        return [(x, True) for x in w] + [(x, x[0] == "ps") for x in r]
+
+    def await_(q, recs):
+        for s, v, snap in recs:
+            if know[q].get(s, 0) >= v:
+                continue
+            if any(o[2].get(s, 0) >= v and (o[0], o[1]) != (s, v) and know[q].get(o[0], 0) < o[1] for o in recs):
+                continue
+            queue[q].wait_ge(T.sem[s], v)
+            know[q][s] = v
+        for s, v, snap in recs:
+            for k in snap:
+                know[q][k] = max(know[q].get(k, 0), snap[k])
+
+    def emit(q, fn, w, r, s=None, n=1):
+        w, r = flat(w), flat(r)
+        recs = {}
+        for (nm, a, b), wr in uses(w, r):
+            for e in acc.get(nm, []):
+                if e[0] < b and a < e[1] and (wr or e[2]):
+                    k = e[3][0]
+                    if k not in recs or recs[k][1] < e[3][1]:
+                        recs[k] = e[3]
+        await_(q, list(recs.values()))
+        s = s or "q" + q
+        fn().then_inc(T.sem[s], n)
+        count[s] = count.get(s, 0) + n
+        snap = dict(know[q])
+        snap[s] = count[s]
+        for (nm, a, b), wr in uses(w, r):
+            l = acc.setdefault(nm, [])
+            if wr:
+                l[:] = [e for e in l if not (a <= e[0] and e[1] <= b)]
+            l.append((a, b, wr, (s, count[s], snap)))
+
+    def copy(out, in_):
+        emit("v", lambda: g.vector.tensor_copy(out[3], in_[3]), [out], [in_])
+
+    def tt(out, a, b, op):
+        emit("v", lambda: g.vector.tensor_tensor(out[3], a[3], b[3], op), [out], [a, b])
+
+    def ts(out, a, s1, op0, s2=None, op1=None):
+        x1 = s1[3] if isinstance(s1, tuple) else s1
+        r = [a] + ([s1] if isinstance(s1, tuple) else [])
+        if op1 is None:
+            emit("v", lambda: g.vector.tensor_scalar(out[3], a[3], x1, None, op0), [out], r)
+        else:
+            emit("v", lambda: g.vector.tensor_scalar(out[3], a[3], x1, s2, op0, op1), [out], r)
+
+    def act(out, in_, func=F.Identity, bias=0.0, scale=1.0):
+        emit("s", lambda: g.scalar.activation(out[3], in_[3], func, bias=bias, scale=scale), [out], [in_])
+
+    def quant(c, p, in_):
+        emit("v", lambda: g.vector.quantize_mx(c[3], p[3], in_[3]), [c, p], [in_])
+
+    def mm(bank, w, wp, x, xp, n):
+        o = V("ps", 512 * bank, 512 * bank + n)
+        emit("t", lambda: g.tensor.matmul_mx(o[3], w[3], wp[3], x[3], xp[3], True, True), [o], [w, wp, x, xp])
+
+    def load(q, name, out, ap):
+        emit(q, lambda: queue[q].dma_start(out[3], ap), [out], [], "ld_" + name, 16)
+
+    def store(ap, in_, q="y"):
+        emit(q, lambda: queue[q].dma_start(ap, in_[3]), [], [in_], "out", 16)
+
+    def iota(out, pattern, cmul, flag=False):
+        emit("g", lambda: g.iota(out[3], pattern, 0, cmul, allow_small_or_imprecise_dtypes=flag), [out], [])
+
+    def scan(out, r):
+        emit("v", lambda: g.vector.tensor_tensor_scan(out[3], row("d0")[3], r[3], 0.0, A.add, A.max), [out], [row("d0"), r])
+
+    def held(name):
+        return V(name, 15, C, 16)
+
+    CP, PM, NUM, QW = V("cp", 0, 1), V("pm", 0, 1), row("num"), V("qw", 0, 24)
+
+    load("s", "pp", V("ppi", 0, 24), T.pp[:])
+    load("y", "u", V("uin", 0, 512), T.u[:])
+    load("s", "pr", V("pri", 0, 72), T.pr[:])
+    load("s", "rf", V("rfi", 0, 24), T.rf[:])
+    load("y", "x", V("xin", 0, 1536), T.x[:])
+    load("y", "wc", bits(V("wq", 0, 512)), T.wc[:])
+    load("y", "ws", V("wp", 0, 512), T.ws[:])
+    load("y", "v", V("vin", 0, 512), T.v[:])
+    ONE, EYE = V("one", 0, 516), V("eye", 0, 516)
+    emit("v", lambda: g.vector.memset(ONE[3], 1.0), [ONE], [])
+    iota(V("pid", 0, 2), [[0, 2]], 1)
+    iota(V("uoi", 0, 16), [[1, 2], [16, 8]], 0)
+    iota(V("q16", 0, 24), [[16, 24]], 0)
+    iota(row("cm"), [[0, 24], [1, 16]], 0)
+    iota(NUM, [[1, C]], 0, True)
+    emit("g", lambda: g.affine_select(EYE[3], ONE[3], [[-1, 516]], A.is_equal, 0.0, 3, 4), [EYE], [ONE])
+    ts(V("pmi", 0, 2), V("pid", 0, 2), 15, A.bitwise_and)
+    copy(V("uo", 0, 16), V("uoi", 0, 16))
+    copy(V("pm", 0, 2), V("pmi", 0, 2))
+    ts(CP, PM, 15.0, A.is_lt, HOLD, A.mult)
+    ts(QW, V("q16", 0, 24), PM, A.add)
+    ts(row("xd"), row("cm"), PM, A.subtract)
+    P, FU, INV, PKU = V("p0", 0, 24), V("f0", 0, 24), V("iu", 0, 24), V("pku", 0, 24)
+    copy(P, V("ppi", 0, 24))
+    ts(row("d1"), row("xd"), 0.0, A.is_equal, -30000.0, A.mult)
+    copy(V("ku", 0, 72), V("pri", 0, 72))
+    copy(FU, V("rfi", 0, 24))
+    ts(row("d2"), row("xd"), 1.0, A.is_equal, HOLD, A.mult)
+    quant(V("uq", 0, 128), V("up", 0, 128), V("uin", 0, 512))
+    UO = V("uo", 0, 16)
+    copy(bits(V("uuq", 0, 256), dt.uint32), ind(bits(V("uq", 0, 128), dt.uint32), UO))
+    copy(V("uup", 0, 256), ind(V("up", 0, 128), UO))
+    tt(row("d0"), row("d1"), row("d2"), A.add)
+    copy(V("ba0", 24, 48), V("ppi", 0, 24))
+    copy(V("ba0", 48, 72), V("rfi", 0, 24))
+    for t in range(3):
+        copy(V("ba%d" % t, 0, 24), QW)
+        tt(V("dd%d" % t, 0, 24), V("pri", 24 * t, 24 * t + 24), QW, A.subtract)
+
+    def candidates(t, P, FU):
+        K = V("ku", 24 * t, 24 * t + 24)
+        act(row("prow"), ind(NUM, P))
+        act(row("pk"), ind(row("prow"), K), bias=-MID)
+        act(row("frow"), ind(NUM, FU))
+        act(row("fk"), ind(row("frow"), K), bias=-MID)
+
+    def differences(t):
+        D, B = "dd%d" % t, "ba%d" % t
+        scan(row("scp"), row("pk"))
+        scan(row("scf"), row("fk"))
+        ts(PKU, held("scp"), CP, A.subtract, MID, A.add)
+        ts(V("pkw", 0, 24), held("scp"), CP, A.subtract, MID, A.add)
+        ts(V("pkw", 24, 48), held("scf"), CP, A.subtract, MID, A.add)
+        tt(V(D, 24, 72), V("pkw", 0, 48), V(B, 24, 72), A.subtract)
+        ts(V("dcp", 0, 72), V(D, 0, 72), CP, A.mult)
+        tt(V("bs", 0, 72), V(B, 0, 72), V("dcp", 0, 72), A.subtract)
+
+    candidates(0, P, FU)
+    quant(V("xq0", 0, C), V("xp0", 0, C), V("xin", 0, 1536))
+    for b in range(4):
+        quant(V("eq", 128 * b, 128 * b + 128), V("ep", 128 * b, 128 * b + 128), V("eye", 3 - b, 515 - b))
+
+    for t in range(3):
+        last = t == 2
+        other = T.cores[rank ^ STEP[t]]
+        eng = topo.engines(core, other)
+        mask = sum(1 << e for e in eng)
+        rid, pnc = topo.addr(other)[:2]
+        X, XP = V("xq%d" % t, 0, C), V("xp%d" % t, 0, C)
+
+        def send(dst, src, s, made):
+            recs = [e[3] for nm, a, b in flat([made]) for e in acc[nm] if e[2] and e[0] < b and a < e[1]]
+            await_("g", recs)
+            g.remote_dma(dst[3], src[3], T.sem[s], T.sem.sent, pnc, rid, mask)
+            count["sent"] = count.get("sent", 0) + len(eng)
+            count[s] = len(eng)
+            acc.setdefault(dst[0], []).append((dst[1], dst[2], True, (s, len(eng), {s: len(eng)})))
+
+        mm(4, V("uuq", 0, 128), V("uup", 0, 128), X, XP, C)
+        mm(5, V("uuq", 128, 256), V("uup", 128, 256), X, XP, C)
+        for b in range(4):
+            mm(b, V("eq", 128 * b, 128 * b + 128), V("ep", 128 * b, 128 * b + 128), X, XP, C)
+        differences(t)
+        act(row("aw"), V("ps", 2048, 2048 + C), F.Sign, bias=-2.0 ** -93)
+        pu, ku = V(P[0], P[1], P[1] + 12), V("pku", 0, 12)
+        pv, kv = V(P[0], P[1] + 12, P[2]), V("pku", 12, 24)
+        copy(V("ar", 0, H), ind(row("aw"), pu))
+        act(V("ar", H, C), ind(row("aw"), pv), F.Copy)
+        tt(V("er", 0, H), ind(row("aw"), ku), V("ar", 0, H), A.is_equal)
+        tt(V("er", H, C), ind(row("aw"), kv), V("ar", H, C), A.is_equal)
+        act(row("bw"), V("ps", 2560, 2560 + C), F.Sign)
+        for b in range(4):
+            act(V("fb", C * b, C * b + C), V("ps", 512 * b, 512 * b + C), F.Copy)
+        scan(row("sc"), row("er"))
+        for i in range(3):
+            tt(V("mu", 24 * i, 24 * i + 24), held("sc"), V("dd%d" % t, 24 * i, 24 * i + 24), A.mult)
+        tt(V("sel", 0, 72), V("mu", 0, 72), V("bs", 0, 72), A.add)
+        copy(V("tu", 0, 72), V("sel", 0, 72))
+        TU, P, CU = V("tu", 0, 24), V("tu", 24, 48), V("tu", 48, 72)
+        act(row("br"), ind(row("bw"), P), bias=-512.0, scale=512.0)
+        for b in range(4):
+            act(V("gb", C * b, C * b + C), ind(V("fb", C * b, C * b + C), P), F.Copy, scale=0.5)
+        tt(V("y1", 0, 24), V("sel", 48, 72), V("sel", 0, 24), A.subtract)
+        copy(row("tr"), ind(NUM, TU))
+        tt(V("yy", 0, 24), V("y1", 0, 24), QW, A.add)
+        tt(row("rr"), ind(row("tr"), CU), row("br"), A.add)
+        ts(V("ni", 0, 24), V("yy", 0, 24), -191.5, A.add, 1.0 / C, A.mult)
+        scan(row("sc2"), row("rr"))
+        ts(V("nf", 0, 24), V("ni", 0, 24), -float(C), A.mult)
+        ts(V("mm", 0, 24), held("sc2"), CP, A.subtract, 0.0, A.is_lt)
+        tt(V("al", 0, 24), V("yy", 0, 24), V("nf", 0, 24), A.add)
+        ts(V("alc", 0, 24), V("al", 0, 24), CP, A.add)
+        tt(V("ma", 0, 24), V("mm", 0, 24), V("alc", 0, 24), A.mult)
+        tt(V("mx", 0, 24), V("ma", 0, 24), held("sc2"), A.max)
+        FU = V("fu%d" % t, 0, 24)
+        ts(FU, V("mx", 0, 24), CP, A.subtract)
+        send(V("lf%d" % t, 0, 24), FU, "af%d" % t, FU)
+
+        def twin(b, h):
+            copy(V("gc", C * b + H * h, C * b + H * h + H), V("gb", C * b + H * h, C * b + H * h + H))
+
+        def mix(b, h):
+            o = V("zt", 768 * h + b, 768 * h + 768, 4)
+            tt(o, ind(V("gb", C * b, C * b + C), V(FU[0], 12 * h, 12 * h + 12)), V("gc", C * b + H * h, C * b + H * h + H), A.add)
+        twin(0, 1)
+        twin(1, 1)
+        mix(0, 1)
+        mix(1, 1)
+        twin(2, 1)
+        twin(0, 0)
+        mix(2, 1)
+        twin(3, 1)
+        mix(0, 0)
+        mix(3, 1)
+        twin(1, 0)
+        UQ, UP = V("zuq%d" % t, 0, H), V("zup%d" % t, 0, H)
+        quant(UQ, UP, V("zt", 768, 1536))
+        send(bits(V("lq%d" % t, 0, H)), bits(UQ), "aq%d" % t, UQ)
+        send(V("lp%d" % t, 0, H), UP, "ap%d" % t, UP)
+        twin(2, 0)
+        mix(1, 0)
+        twin(3, 0)
+        mix(2, 0)
+        mix(3, 0)
+        quant(V("zlq", 0, H), V("zlp", 0, H), V("zt", 0, 768))
+        if t == 0:
+            P0 = V("p0", 0, 24)
+            iv = ind(row("iv0"), P0)
+            emit("v", lambda: g.vector.tensor_copy(iv[3], NUM[3]), [row("iv0")], [NUM, P0])
+            scan(row("sc3"), row("iv0"))
+            ts(INV, held("sc3"), CP, A.subtract)
+        for b in range(4):
+            mm(b, V("wq", 128 * b, 128 * b + 128), V("wp", 128 * b, 128 * b + 128), V("zlq", 0, H), V("zlp", 0, H), H)
+        act(row("ir"), ind(row("tr"), INV), bias=-MID)
+        act(row("fs"), ind(NUM, V("lf%d" % t, 0, 24)))
+        act(row("ef"), ind(row("fs"), FU))
+        scan(row("sc3"), row("ir"))
+        ts(INV, held("sc3"), CP, A.subtract, MID, A.add)
+        if not last:
+            copy(V("ba%d" % (t + 1), 24, 48), V("sel", 24, 48))
+            ts(V("ba%d" % (t + 1), 48, 72), V("mx", 0, 24), CP, A.subtract)
+        act(row("ej"), ind(row("ef"), INV), bias=-MID)
+        for b in range(4):
+            ts(V("bb", C * b, C * b + H), V("ps", 512 * b, 512 * b + H), 0.03125, A.mult)
+        scan(row("sc4"), row("ej"))
+        ts(V("eu", 0, 24), held("sc4"), CP, A.subtract, MID, A.add)
+        for b in range(4):
+            mm(4 + b, V("wq", 128 * b, 128 * b + 128), V("wp", 128 * b, 128 * b + 128), V("lq%d" % t, 0, H), V("lp%d" % t, 0, H), H)
+        for b in range(4):
+            act(V("bb", C * b + H, C * b + C), V("ps", 2048 + 512 * b, 2048 + 512 * b + H), F.Copy, scale=0.03125)
+        for b in range(4):
+            tt(V("xt", b, 1536, 4), ind(V("bb", C * b, C * b + C), V("eu", 0, 24)), V("fb", C * b, C * b + C), A.add)
+        if last:
+            act(row("prow"), ind(NUM, P))
+            act(row("frow"), ind(NUM, FU))
+            store(T.pf[:, 0:C], ("prow", 0, C, T.prow[0:128:16, :]))
+            store(T.pf[:, C:2 * C], ("frow", 0, C, T.frow[0:128:16, :]))
+            quant(V("vq", 0, 128), V("vp", 0, 128), V("vin", 0, 512))
+        else:
+            candidates(t + 1, P, FU)
+        quant(V("xq%d" % (t + 1), 0, C), V("xp%d" % (t + 1), 0, C), V("xt", 0, 1536))
+
+    X, XP = V("xq3", 0, C), V("xp3", 0, C)
+    mm(0, V("vq", 0, 128), V("vp", 0, 128), X, XP, C)
+    store(T.oc[:], bits(X))
+    for k in range(4):
+        store(T.osc[4 * k:4 * k + 4, :], ("xp3", 0, C, T.xp3[32 * k:32 * k + 4, :]), "s" if k % 2 else "y")
+    ts(row("yo"), V("ps", 0, C), 1.0, A.mult)
+    store(T.y[:], row("yo"))
+    for s in count:
+        if know["g"].get(s, 0) < count[s]:
+            g.wait_ge(T.sem[s], count[s])

@@ -10,18 +10,18 @@ for _n, _c, _d in (
         [("xin", 1536, BF), ("uin", 512, BF), ("vin", 512, BF), ("ppi", 24, "int32"), ("rfi", 24, "int32"), ("pri", 72, "int32")]
         + [("wq", 512, CODE), ("wp", 512, "uint8"), ("uq", 128, CODE), ("up", 128, "uint8"), ("uuq", 256, CODE), ("uup", 256, "uint8")]
         + [("vq", 128, CODE), ("vp", 128, "uint8"), ("eq", 512, CODE), ("ep", 512, "uint8"), ("zlq", H, CODE), ("zlp", H, "uint8")]
-        + [("one", 516, BF), ("eye", 516, BF), ("uoi", 16, "int32"), ("uo", 16, "uint16"), ("cm", C, "int32"), ("pid", 2, "int32")]
-        + [("pmi", 2, "int32"), ("pm", 2, FL), ("cp", 1, FL), ("q16", 24, "int32"), ("qw", 24, FL), ("num", C, FL), ("xd", C, FL)]
+        + [("one", 516, BF), ("eye", 516, BF), ("uoi", 16, "int32"), ("uo", 16, "uint16"), ("cm", C, BF), ("pid", 2, "int32")]
+        + [("pmi", 2, "int32"), ("pm", 2, FL), ("cp", 1, FL), ("q16", 24, "int32"), ("qw", 24, FL), ("num", C, FL), ("xd", C, BF)]
         + [("d1", C, HF), ("d2", C, HF), ("d0", C, HF)]
         + [(k, 1536, BF) for k in ("fb", "gb", "gc", "bb", "zt", "xt")]
-        + [(k, C, BF) for k in ("aw", "ar", "bw", "br", "pk", "fk", "ir", "ej")]
-        + [(k, C, HF) for k in ("er", "rr", "sc", "sc2", "sc3", "sc4", "scp", "scf")]
+        + [(k, C, BF) for k in ("aw", "ar", "bw", "br", "pk", "fk", "ir", "ej", "hr", "b3")]
+        + [(k, C, HF) for k in ("er", "rr", "sc", "sc2", "sc3", "sc4", "sc5", "scb", "scp", "scf")]
         + [(k, C, FL) for k in ("iv0", "tr", "prow", "frow", "fs", "ef", "yo")]
-        + [(k, 72, FL) for k in ("dcp", "bs", "mu", "sel")]
-        + [(k, 24, FL) for k in ("yy", "y1", "nf", "al", "alc", "mm", "ma", "mx")] + [("pkw", 48, FL), ("ni", 24, "int32")]
-        + [("ku", 72, "uint16"), ("tu", 72, "uint16")] + [(k, 24, "uint16") for k in ("p0", "f0", "iu", "eu", "pku")]
+        + [(k, 96, FL) for k in ("dcp", "bs", "mu", "sel")]
+        + [(k, 24, FL) for k in ("nf", "al", "alc", "mm", "ma", "mx")] + [("pkw", 48, FL), ("ni", 24, "int32")]
+        + [("ku", 72, "uint16"), ("tu", 72, "uint16")] + [(k, 24, "uint16") for k in ("p0", "f0", "iu", "eu", "hu", "pku")]
         + [("xq%d" % t, C, CODE) for t in range(4)] + [("xp%d" % t, C, "uint8") for t in range(4)]
-        + [("%s%d" % (k, t), 72, FL) for k in ("dd", "ba") for t in range(3)]
+        + [("%s%d" % (k, t), 96, FL) for k in ("dd", "ba") for t in range(3)]
         + [("%s%d" % (k, t), 24, "uint16") for k in ("fu", "lf") for t in range(3)]
         + [("%s%d" % (k, t), H, CODE) for k in ("zuq", "lq") for t in range(3)]
         + [("%s%d" % (k, t), H, "uint8") for k in ("zup", "lp") for t in range(3)]):
@@ -40,6 +40,9 @@ def rank_program(g, core, T, topo):
     def V(name, lo, hi, step=1):
         return (name, lo, hi, T[name][:, lo:hi] if step == 1 else T[name][:, lo:hi:step])
 
+    def lane(name, b, lo, hi):
+        return ("%s%d" % (name, b), 4 * lo, 4 * hi, T[name][:, 4 * lo + b:4 * hi:4])
+
     def row(name):
         return V(name, 0, C)
 
@@ -52,7 +55,10 @@ def rank_program(g, core, T, topo):
     def flat(vs):
         r = []
         for v in vs:
-            r += [v[1], v[2]] if v[0] == "*" else [v]
+            if v[0] in ("zt", "xt"):
+                r += [("%s%d" % (v[0], b), v[1], v[2], None) for b in range(4)]
+            else:
+                r += [v[1], v[2]] if v[0] == "*" else [v]
         return [(n, a, b) if n != "ps" else (n, a // 512 * 512, -(-b // 512) * 512) for n, a, b, _ in r]
 
     def uses(w, r):
@@ -144,55 +150,65 @@ def rank_program(g, core, T, topo):
     emit("v", lambda: g.vector.memset(ONE[3], 1.0), [ONE], [])
     iota(V("pid", 0, 2), [[0, 2]], 1)
     iota(V("uoi", 0, 16), [[1, 2], [16, 8]], 0)
-    iota(V("q16", 0, 24), [[16, 24]], 0)
-    iota(row("cm"), [[0, 24], [1, 16]], 0)
+    iota(row("cm"), [[0, 24], [1, 16]], 0, True)
     iota(NUM, [[1, C]], 0, True)
     emit("g", lambda: g.affine_select(EYE[3], ONE[3], [[-1, 516]], A.is_equal, 0.0, 3, 4), [EYE], [ONE])
+    iota(V("q16", 0, 24), [[16, 24]], 0)
     ts(V("pmi", 0, 2), V("pid", 0, 2), 15, A.bitwise_and)
     copy(V("uo", 0, 16), V("uoi", 0, 16))
     copy(V("pm", 0, 2), V("pmi", 0, 2))
     ts(CP, PM, 15.0, A.is_lt, HOLD, A.mult)
-    ts(QW, V("q16", 0, 24), PM, A.add)
     ts(row("xd"), row("cm"), PM, A.subtract)
     P, FU, INV, PKU = V("p0", 0, 24), V("f0", 0, 24), V("iu", 0, 24), V("pku", 0, 24)
-    copy(P, V("ppi", 0, 24))
     ts(row("d1"), row("xd"), 0.0, A.is_equal, -30000.0, A.mult)
+    ts(row("d2"), row("xd"), 1.0, A.is_equal, HOLD, A.mult)
+    copy(P, V("ppi", 0, 24))
     copy(V("ku", 0, 72), V("pri", 0, 72))
     copy(FU, V("rfi", 0, 24))
-    ts(row("d2"), row("xd"), 1.0, A.is_equal, HOLD, A.mult)
+    iv = ind(row("iv0"), P)
+    emit("v", lambda: g.vector.tensor_copy(iv[3], NUM[3]), [row("iv0")], [NUM, P])
     quant(V("uq", 0, 128), V("up", 0, 128), V("uin", 0, 512))
     UO = V("uo", 0, 16)
-    copy(bits(V("uuq", 0, 256), dt.uint32), ind(bits(V("uq", 0, 128), dt.uint32), UO))
-    copy(V("uup", 0, 256), ind(V("up", 0, 128), UO))
-    tt(row("d0"), row("d1"), row("d2"), A.add)
-    copy(V("ba0", 24, 48), V("ppi", 0, 24))
-    copy(V("ba0", 48, 72), V("rfi", 0, 24))
-    for t in range(3):
-        copy(V("ba%d" % t, 0, 24), QW)
-        tt(V("dd%d" % t, 0, 24), V("pri", 24 * t, 24 * t + 24), QW, A.subtract)
 
-    def candidates(t, P, FU):
+    def candidates(t, P, FU, part):
         K = V("ku", 24 * t, 24 * t + 24)
-        act(row("prow"), ind(NUM, P))
-        act(row("pk"), ind(row("prow"), K), bias=-MID)
-        act(row("frow"), ind(NUM, FU))
-        act(row("fk"), ind(row("frow"), K), bias=-MID)
+        if part == 0:
+            act(row("prow"), ind(NUM, P))
+        if part == 1:
+            act(row("pk"), ind(row("prow"), K), bias=-MID)
 
     def differences(t):
         D, B = "dd%d" % t, "ba%d" % t
-        scan(row("scp"), row("pk"))
+        if t:
+            scan(row("scp"), row("pk"))
+            ts(PKU, held("scp"), CP, A.subtract, MID, A.add)
         scan(row("scf"), row("fk"))
-        ts(PKU, held("scp"), CP, A.subtract, MID, A.add)
         ts(V("pkw", 0, 24), held("scp"), CP, A.subtract, MID, A.add)
         ts(V("pkw", 24, 48), held("scf"), CP, A.subtract, MID, A.add)
         tt(V(D, 24, 72), V("pkw", 0, 48), V(B, 24, 72), A.subtract)
-        ts(V("dcp", 0, 72), V(D, 0, 72), CP, A.mult)
-        tt(V("bs", 0, 72), V(B, 0, 72), V("dcp", 0, 72), A.subtract)
+        ts(V(B, 72, 96), V(B, 48, 72), 0.0, A.add)
+        tt(V(D, 72, 96), V(D, 48, 72), V(D, 0, 24), A.subtract)
+        ts(V("dcp", 0, 96), V(D, 0, 96), CP, A.mult)
+        tt(V("bs", 0, 96), V(B, 0, 96), V("dcp", 0, 96), A.subtract)
 
-    candidates(0, P, FU)
+    candidates(0, P, FU, 0)
+    copy(bits(V("uuq", 0, 256), dt.uint32), ind(bits(V("uq", 0, 128), dt.uint32), UO))
+    uup, upw = V("uup", 0, 256), ind(V("up", 0, 128), UO)
+    emit("s", lambda: g.scalar.activation(uup[3], upw[3], F.Copy), [uup], [upw])
+    candidates(0, P, FU, 1)
+    act(row("frow"), ind(NUM, FU))
     quant(V("xq0", 0, C), V("xp0", 0, C), V("xin", 0, 1536))
+    tt(row("d0"), row("d1"), row("d2"), A.add)
+    ts(QW, V("q16", 0, 24), PM, A.add)
+    scan(row("scp"), row("pk"))
     for b in range(4):
         quant(V("eq", 128 * b, 128 * b + 128), V("ep", 128 * b, 128 * b + 128), V("eye", 3 - b, 515 - b))
+    copy(V("ba0", 24, 48), V("ppi", 0, 24))
+    copy(V("ba0", 48, 72), V("rfi", 0, 24))
+
+    def own(t):
+        copy(V("ba%d" % t, 0, 24), QW)
+        tt(V("dd%d" % t, 0, 24), V("pri", 24 * t, 24 * t + 24), QW, A.subtract)
 
     for t in range(3):
         last = t == 2
@@ -214,113 +230,171 @@ def rank_program(g, core, T, topo):
         mm(5, V("uuq", 128, 256), V("uup", 128, 256), X, XP, C)
         for b in range(4):
             mm(b, V("eq", 128 * b, 128 * b + 128), V("ep", 128 * b, 128 * b + 128), X, XP, C)
-        differences(t)
+        if t:
+            differences(t)
+        else:
+            ts(PKU, held("scp"), CP, A.subtract, MID, A.add)
+            own(0)
         act(row("aw"), V("ps", 2048, 2048 + C), F.Sign, bias=-2.0 ** -93)
         pu, ku = V(P[0], P[1], P[1] + 12), V("pku", 0, 12)
         pv, kv = V(P[0], P[1] + 12, P[2]), V("pku", 12, 24)
-        copy(V("ar", 0, H), ind(row("aw"), pu))
+        act(V("ar", 0, H), ind(row("aw"), pu), F.Copy)
         act(V("ar", H, C), ind(row("aw"), pv), F.Copy)
         tt(V("er", 0, H), ind(row("aw"), ku), V("ar", 0, H), A.is_equal)
         tt(V("er", H, C), ind(row("aw"), kv), V("ar", H, C), A.is_equal)
+        if t == 0:
+            act(row("fk"), ind(row("frow"), V("ku", 0, 24)), bias=-MID)
+            differences(0)
         act(row("bw"), V("ps", 2560, 2560 + C), F.Sign)
-        for b in range(4):
+        for b in range(2):
             act(V("fb", C * b, C * b + C), V("ps", 512 * b, 512 * b + C), F.Copy)
         scan(row("sc"), row("er"))
-        for i in range(3):
+        for i in range(4):
             tt(V("mu", 24 * i, 24 * i + 24), held("sc"), V("dd%d" % t, 24 * i, 24 * i + 24), A.mult)
         tt(V("sel", 0, 72), V("mu", 0, 72), V("bs", 0, 72), A.add)
+        tt(V("sel", 72, 96), V("mu", 72, 96), V("bs", 72, 96), A.add)
         copy(V("tu", 0, 72), V("sel", 0, 72))
         TU, P, CU = V("tu", 0, 24), V("tu", 24, 48), V("tu", 48, 72)
-        act(row("br"), ind(row("bw"), P), bias=-512.0, scale=512.0)
-        for b in range(4):
+        act(row("br"), ind(row("bw"), P), F.Relu)
+        for b in (2, 3):
+            act(V("fb", C * b, C * b + C), V("ps", 512 * b, 512 * b + C), F.Copy)
+        for b in range(3):
             act(V("gb", C * b, C * b + C), ind(V("fb", C * b, C * b + C), P), F.Copy, scale=0.5)
-        tt(V("y1", 0, 24), V("sel", 48, 72), V("sel", 0, 24), A.subtract)
+        act(V("gb", 3 * C + H, 4 * C), ind(V("fb", 3 * C, 4 * C), V("tu", 36, 48)), F.Copy, scale=0.5)
+        ts(V("ni", 0, 24), V("sel", 72, 96), -191.5, A.add, 1.0 / C, A.mult)
         copy(row("tr"), ind(NUM, TU))
-        tt(V("yy", 0, 24), V("y1", 0, 24), QW, A.add)
-        tt(row("rr"), ind(row("tr"), CU), row("br"), A.add)
-        ts(V("ni", 0, 24), V("yy", 0, 24), -191.5, A.add, 1.0 / C, A.mult)
-        scan(row("sc2"), row("rr"))
         ts(V("nf", 0, 24), V("ni", 0, 24), -float(C), A.mult)
-        ts(V("mm", 0, 24), held("sc2"), CP, A.subtract, 0.0, A.is_lt)
-        tt(V("al", 0, 24), V("yy", 0, 24), V("nf", 0, 24), A.add)
+        tt(row("rr"), ind(row("tr"), CU), row("br"), A.mult)
+        tt(V("al", 0, 24), V("sel", 72, 96), V("nf", 0, 24), A.add)
+        scan(row("scb"), row("br"))
         ts(V("alc", 0, 24), V("al", 0, 24), CP, A.add)
+        ts(V("mm", 0, 24), held("scb"), CP, A.subtract, 0.5, A.is_lt)
+        scan(row("sc2"), row("rr"))
         tt(V("ma", 0, 24), V("mm", 0, 24), V("alc", 0, 24), A.mult)
+        if not last:
+            copy(V("ba%d" % (t + 1), 24, 48), V("sel", 24, 48))
         tt(V("mx", 0, 24), V("ma", 0, 24), held("sc2"), A.max)
         FU = V("fu%d" % t, 0, 24)
         ts(FU, V("mx", 0, 24), CP, A.subtract)
+        if t == 0:
+            scan(row("sc3"), row("iv0"))
+            ts(INV, held("sc3"), CP, A.subtract)
+            own(1)
+            own(2)
         send(V("lf%d" % t, 0, 24), FU, "af%d" % t, FU)
 
         def twin(b, h):
             copy(V("gc", C * b + H * h, C * b + H * h + H), V("gb", C * b + H * h, C * b + H * h + H))
 
         def mix(b, h):
-            o = V("zt", 768 * h + b, 768 * h + 768, 4)
+            o = lane("zt", b, H * h, H * h + H)
             tt(o, ind(V("gb", C * b, C * b + C), V(FU[0], 12 * h, 12 * h + 12)), V("gc", C * b + H * h, C * b + H * h + H), A.add)
+        ts(V("gb", 3 * C, 3 * C + H), ind(V("fb", 3 * C, 4 * C), V("tu", 24, 36)), 0.5, A.mult)
         twin(0, 1)
         twin(1, 1)
         mix(0, 1)
         mix(1, 1)
         twin(2, 1)
-        twin(0, 0)
         mix(2, 1)
         twin(3, 1)
-        mix(0, 0)
         mix(3, 1)
-        twin(1, 0)
         UQ, UP = V("zuq%d" % t, 0, H), V("zup%d" % t, 0, H)
         quant(UQ, UP, V("zt", 768, 1536))
         send(bits(V("lq%d" % t, 0, H)), bits(UQ), "aq%d" % t, UQ)
         send(V("lp%d" % t, 0, H), UP, "ap%d" % t, UP)
-        twin(2, 0)
-        mix(1, 0)
-        twin(3, 0)
-        mix(2, 0)
-        mix(3, 0)
-        quant(V("zlq", 0, H), V("zlp", 0, H), V("zt", 0, 768))
-        if t == 0:
-            P0 = V("p0", 0, 24)
-            iv = ind(row("iv0"), P0)
-            emit("v", lambda: g.vector.tensor_copy(iv[3], NUM[3]), [row("iv0")], [NUM, P0])
-            scan(row("sc3"), row("iv0"))
-            ts(INV, held("sc3"), CP, A.subtract)
-        for b in range(4):
-            mm(b, V("wq", 128 * b, 128 * b + 128), V("wp", 128 * b, 128 * b + 128), V("zlq", 0, H), V("zlp", 0, H), H)
         act(row("ir"), ind(row("tr"), INV), bias=-MID)
-        act(row("fs"), ind(NUM, V("lf%d" % t, 0, 24)))
-        act(row("ef"), ind(row("fs"), FU))
         scan(row("sc3"), row("ir"))
+        twin(0, 0)
         ts(INV, held("sc3"), CP, A.subtract, MID, A.add)
-        if not last:
-            copy(V("ba%d" % (t + 1), 24, 48), V("sel", 24, 48))
-            ts(V("ba%d" % (t + 1), 48, 72), V("mx", 0, 24), CP, A.subtract)
-        act(row("ej"), ind(row("ef"), INV), bias=-MID)
-        for b in range(4):
-            ts(V("bb", C * b, C * b + H), V("ps", 512 * b, 512 * b + H), 0.03125, A.mult)
-        scan(row("sc4"), row("ej"))
-        ts(V("eu", 0, 24), held("sc4"), CP, A.subtract, MID, A.add)
-        for b in range(4):
-            mm(4 + b, V("wq", 128 * b, 128 * b + 128), V("wp", 128 * b, 128 * b + 128), V("lq%d" % t, 0, H), V("lp%d" % t, 0, H), H)
-        for b in range(4):
-            act(V("bb", C * b + H, C * b + C), V("ps", 2048 + 512 * b, 2048 + 512 * b + H), F.Copy, scale=0.03125)
-        for b in range(4):
-            tt(V("xt", b, 1536, 4), ind(V("bb", C * b, C * b + C), V("eu", 0, 24)), V("fb", C * b, C * b + C), A.add)
-        if last:
+        if t == 0:
             act(row("prow"), ind(NUM, P))
             act(row("frow"), ind(NUM, FU))
-            store(T.pf[:, 0:C], ("prow", 0, C, T.prow[0:128:16, :]))
-            store(T.pf[:, C:2 * C], ("frow", 0, C, T.frow[0:128:16, :]))
-            quant(V("vq", 0, 128), V("vp", 0, 128), V("vin", 0, 512))
+            act(row("hr"), ind(row("frow"), INV), bias=-MID)
+            candidates(1, P, FU, 1)
+            act(row("fs"), ind(NUM, V("lf0", 0, 24)))
         else:
-            candidates(t + 1, P, FU)
-        quant(V("xq%d" % (t + 1), 0, C), V("xp%d" % (t + 1), 0, C), V("xt", 0, 1536))
+            act(row("prow"), ind(NUM, P))
+            act(row("fs"), ind(NUM, V("lf%d" % t, 0, 24)))
+            act(row("ef"), ind(row("fs"), FU))
+            act(row("ej"), ind(row("ef"), INV), bias=-MID)
+            if not last:
+                candidates(t + 1, P, FU, 1)
+            else:
+                act(row("frow"), ind(NUM, FU))
+        for b in (1, 2, 3):
+            twin(b, 0)
+        for b in range(4):
+            mix(b, 0)
+            if t == 0 and b == 1:
+                scan(row("sc5"), row("hr"))
+                ts(V("hu", 0, 24), held("sc5"), CP, A.subtract, MID, A.add)
+                act(row("ej"), ind(row("fs"), V("hu", 0, 24)), bias=-MID)
+        quant(V("zlq", 0, H), V("zlp", 0, H), V("zt", 0, 768))
+        low, up = (0, 1, 2, 5), (4, 6, 7, 0)
 
-    X, XP = V("xq3", 0, C), V("xp3", 0, C)
-    mm(0, V("vq", 0, 128), V("vp", 0, 128), X, XP, C)
-    store(T.oc[:], bits(X))
+        def layer(b, h):
+            x = (V("lq%d" % t, 0, H), V("lp%d" % t, 0, H)) if h else (V("zlq", 0, H), V("zlp", 0, H))
+            mm((low, up)[h][b], V("wq", 128 * b, 128 * b + 128), V("wp", 128 * b, 128 * b + 128), x[0], x[1], H)
+
+        def cast(b, h):
+            o, i = V("bb", C * b + H * h, C * b + H * h + H), 512 * (low, up)[h][b]
+            if b == 0:
+                ts(o, V("ps", i, i + H), 0.03125, A.mult)
+            else:
+                act(o, V("ps", i, i + H), F.Copy, scale=0.03125)
+        layer(0, 0)
+        layer(1, 0)
+        layer(0, 1)
+        layer(1, 1)
+        if t:
+            scan(row("sc4"), row("ej"))
+        cast(0, 0)
+        cast(1, 0)
+        if not t:
+            scan(row("sc4"), row("ej"))
+        ts(V("eu", 0, 24), held("sc4"), CP, A.subtract, MID, A.add)
+        if not last:
+            ts(V("ba%d" % (t + 1), 48, 72), V("mx", 0, 24), CP, A.subtract)
+        cast(0, 1)
+        cast(1, 1)
+        for b in (2, 3):
+            for h in (0, 1):
+                layer(b, h)
+                cast(b, h)
+
+        def state(b, h=None):
+            lo, hi = (0, C) if h is None else (H * h, H * h + H)
+            tt(lane("xt", b, lo, hi), ind(V("bb", C * b, C * b + C), V("eu", lo // 16, hi // 16)), V("fb", C * b + lo, C * b + hi), A.add)
+        if not last:
+            act(row("b3"), ind(V("bb", 3 * C, 4 * C), V("eu", 0, 24)), F.Copy)
+            for b in range(3):
+                state(b)
+            tt(lane("xt", 3, 0, C), row("b3"), V("ps", 1536, 1536 + C), A.add)
+            if t:
+                act(row("frow"), ind(NUM, FU))
+            act(row("fk"), ind(row("frow"), V("ku", 24 * t + 24, 24 * t + 48)), bias=-MID)
+            quant(V("xq%d" % (t + 1), 0, C), V("xp%d" % (t + 1), 0, C), V("xt", 0, 1536))
+    store(T.pf[:, 0:C], ("prow", 0, C, T.prow[0:128:16, :]))
+    store(T.pf[:, C:2 * C], ("frow", 0, C, T.frow[0:128:16, :]))
+    quant(V("vq", 0, 128), V("vp", 0, 128), V("vin", 0, 512))
+    for b, h in ((0, 0), (0, 1), (1, 0), (1, 1), (2, 0), (3, 0)):
+        state(b, h)
+
+    def finish(h):
+        X, XP = V("xq3", H * h, H * h + H), V("xp3", H * h, H * h + H)
+        quant(X, XP, V("xt", 768 * h, 768 * h + 768))
+        mm(4 + h, V("vq", 0, 128), V("vp", 0, 128), X, XP, H)
+        store(T.oc[:, 768 * h:768 * h + 768], bits(X))
+    finish(0)
+    act(V("yo", 0, H), V("ps", 2048, 2048 + H), F.Copy)
+    store(T.y[:, 0:H], V("yo", 0, H), "s")
+    state(2, 1)
+    state(3, 1)
+    finish(1)
     for k in range(4):
-        store(T.osc[4 * k:4 * k + 4, :], ("xp3", 0, C, T.xp3[32 * k:32 * k + 4, :]), "s" if k % 2 else "y")
-    ts(row("yo"), V("ps", 0, C), 1.0, A.mult)
-    store(T.y[:], row("yo"))
+        store(T.osc[4 * k:4 * k + 4, :], ("xp3", 0, C, T.xp3[32 * k:32 * k + 4, :]), "y" if k % 2 else "s")
+    ts(V("yo", H, C), V("ps", 2560, 2560 + H), 1.0, A.mult)
+    store(T.y[:, H:C], V("yo", H, C))
     for s in count:
         if know["g"].get(s, 0) < count[s]:
             g.wait_ge(T.sem[s], count[s])

from concourse.mybir import dt, AluOpType as A, ActivationFunctionType as F

C, H, STEP = 384, 192, [1, 2, 4]
HOLD = 1408.0
MID = 192.0
BF, HF, FL, CODE = "bfloat16", "float16", "float32", "float8_e4m3fn_x4"

SCRATCH = {"ps": ("psum", [128, 4096], "float32")}
for _n, _c, _d in (
        [("xin", 1536, BF), ("uin", 512, BF), ("vin", 512, BF), ("ppi", 24, "int32"), ("rfi", 24, "int32"), ("pri", 72, "int32")]
        + [("wq", 512, CODE), ("wp", 512, "uint8"), ("uq", 128, CODE), ("up", 128, "uint8"), ("uuq", 256, CODE), ("uup", 256, "uint8")]
        + [("vq", 128, CODE), ("vp", 128, "uint8"), ("eq", 512, CODE), ("ep", 512, "uint8"), ("zlq", H, CODE), ("zlp", H, "uint8")]
        + [("one", 516, BF), ("eye", 516, BF), ("uoi", 16, "int32"), ("uo", 16, "uint16"), ("cm", C, BF), ("pid", 2, "int32")]
        + [("pmi", 2, "int32"), ("pm", 2, FL), ("cp", 1, FL), ("q16", 24, "int32"), ("qw", 24, FL), ("num", C, FL), ("xd", C, BF)]
        + [("d1", C, HF), ("d2", C, HF), ("d0", C, HF)]
        + [(k, 1536, BF) for k in ("fb", "gb", "gc", "bb", "zt", "xt")]
        + [(k, C, BF) for k in ("aw", "ar", "bw", "br", "pk", "fk", "ir", "ej", "hr", "b3")]
        + [(k, C, HF) for k in ("er", "rr", "sc", "sc2", "sc3", "sc4", "sc5", "scb", "scp", "scf")]
        + [(k, C, FL) for k in ("iv0", "tr", "prow", "frow", "fs", "ef", "yo")]
        + [(k, 96, FL) for k in ("dcp", "bs", "mu", "sel")]
        + [(k, 24, FL) for k in ("nf", "al", "alc", "mm", "ma", "mx")] + [("pkw", 48, FL), ("ni", 24, "int32")]
        + [("ku", 72, "uint16"), ("tu", 72, "uint16")] + [(k, 24, "uint16") for k in ("p0", "f0", "iu", "eu", "hu", "pku")]
        + [("xq%d" % t, C, CODE) for t in range(4)] + [("xp%d" % t, C, "uint8") for t in range(4)]
        + [("%s%d" % (k, t), 96, FL) for k in ("dd", "ba") for t in range(3)]
        + [("%s%d" % (k, t), 24, "uint16") for k in ("fu", "lf") for t in range(3)]
        + [("%s%d" % (k, t), H, CODE) for k in ("zuq", "lq") for t in range(3)]
        + [("%s%d" % (k, t), H, "uint8") for k in ("zup", "lp") for t in range(3)]):
    SCRATCH[_n] = ("sbuf", [128, _c], _d)
LOADS = ["x", "u", "v", "pp", "rf", "pr", "wc", "ws"]
SEMAPHORES = ["qv", "qs", "qt", "qg", "sent", "out"] + ["ld_" + k for k in LOADS] + ["%s%d" % (k, t) for k in ("af", "aq", "ap") for t in range(3)]


def rank_program(g, core, T, topo):
    rank = T.rank_of(core)
    if rank is None:
        return
    queue = {"v": g.vector, "s": g.scalar, "t": g.tensor, "g": g, "y": g.sync}
    count, know, acc = {}, {k: {} for k in queue}, {}

    def V(name, lo, hi, step=1):
        return (name, lo, hi, T[name][:, lo:hi] if step == 1 else T[name][:, lo:hi:step])

    def lane(name, b, lo, hi):
        return ("%s%d" % (name, b), 4 * lo, 4 * hi, T[name][:, 4 * lo + b:4 * hi:4])

    def row(name):
        return V(name, 0, C)

    def bits(v, d=dt.uint8):
        return (v[0], v[1], v[2], v[3].bitcast(d))

    def ind(win, off):
        return ("*", win, off, win[3].indirect(off[3]))

    def flat(vs):
        r = []
        for v in vs:
            if v[0] in ("zt", "xt"):
                r += [("%s%d" % (v[0], b), v[1], v[2], None) for b in range(4)]
            else:
                r += [v[1], v[2]] if v[0] == "*" else [v]
        return [(n, a, b) if n != "ps" else (n, a // 512 * 512, -(-b // 512) * 512) for n, a, b, _ in r]

    def uses(w, r):
        return [(x, True) for x in w] + [(x, x[0] == "ps") for x in r]

    def await_(q, recs):
        for s, v, snap in recs:
            if know[q].get(s, 0) >= v:
                continue
            if any(o[2].get(s, 0) >= v and (o[0], o[1]) != (s, v) and know[q].get(o[0], 0) < o[1] for o in recs):
                continue
            queue[q].wait_ge(T.sem[s], v)
            know[q][s] = v
        for s, v, snap in recs:
            for k in snap:
                know[q][k] = max(know[q].get(k, 0), snap[k])

    def emit(q, fn, w, r, s=None, n=1):
        w, r = flat(w), flat(r)
        recs = {}
        for (nm, a, b), wr in uses(w, r):
            for e in acc.get(nm, []):
                if e[0] < b and a < e[1] and (wr or e[2]):
                    k = e[3][0]
                    if k not in recs or recs[k][1] < e[3][1]:
                        recs[k] = e[3]
        await_(q, list(recs.values()))
        s = s or "q" + q
        fn().then_inc(T.sem[s], n)
        count[s] = count.get(s, 0) + n
        snap = dict(know[q])
        snap[s] = count[s]
        for (nm, a, b), wr in uses(w, r):
            l = acc.setdefault(nm, [])
            if wr:
                l[:] = [e for e in l if not (a <= e[0] and e[1] <= b)]
            l.append((a, b, wr, (s, count[s], snap)))

    def copy(out, in_):
        emit("v", lambda: g.vector.tensor_copy(out[3], in_[3]), [out], [in_])

    def tt(out, a, b, op):
        emit("v", lambda: g.vector.tensor_tensor(out[3], a[3], b[3], op), [out], [a, b])

    def ts(out, a, s1, op0, s2=None, op1=None):
        x1 = s1[3] if isinstance(s1, tuple) else s1
        r = [a] + ([s1] if isinstance(s1, tuple) else [])
        if op1 is None:
            emit("v", lambda: g.vector.tensor_scalar(out[3], a[3], x1, None, op0), [out], r)
        else:
            emit("v", lambda: g.vector.tensor_scalar(out[3], a[3], x1, s2, op0, op1), [out], r)

    def act(out, in_, func=F.Identity, bias=0.0, scale=1.0):
        emit("s", lambda: g.scalar.activation(out[3], in_[3], func, bias=bias, scale=scale), [out], [in_])

    def quant(c, p, in_):
        emit("v", lambda: g.vector.quantize_mx(c[3], p[3], in_[3]), [c, p], [in_])

    def mm(bank, w, wp, x, xp, n):
        o = V("ps", 512 * bank, 512 * bank + n)
        emit("t", lambda: g.tensor.matmul_mx(o[3], w[3], wp[3], x[3], xp[3], True, True), [o], [w, wp, x, xp])

    def load(q, name, out, ap):
        emit(q, lambda: queue[q].dma_start(out[3], ap), [out], [], "ld_" + name, 16)

    def store(ap, in_, q="y"):
        emit(q, lambda: queue[q].dma_start(ap, in_[3]), [], [in_], "out", 16)

    def iota(out, pattern, cmul, flag=False):
        emit("g", lambda: g.iota(out[3], pattern, 0, cmul, allow_small_or_imprecise_dtypes=flag), [out], [])

    def scan(out, r):
        emit("v", lambda: g.vector.tensor_tensor_scan(out[3], row("d0")[3], r[3], 0.0, A.add, A.max), [out], [row("d0"), r])

    def held(name):
        return V(name, 15, C, 16)

    CP, PM, NUM, QW = V("cp", 0, 1), V("pm", 0, 1), row("num"), V("qw", 0, 24)

    load("s", "pp", V("ppi", 0, 24), T.pp[:])
    load("y", "u", V("uin", 0, 512), T.u[:])
    load("s", "pr", V("pri", 0, 72), T.pr[:])
    load("s", "rf", V("rfi", 0, 24), T.rf[:])
    load("y", "x", V("xin", 0, 1536), T.x[:])
    load("y", "wc", bits(V("wq", 0, 512)), T.wc[:])
    load("y", "ws", V("wp", 0, 512), T.ws[:])
    load("y", "v", V("vin", 0, 512), T.v[:])
    ONE, EYE = V("one", 0, 516), V("eye", 0, 516)
    emit("v", lambda: g.vector.memset(ONE[3], 1.0), [ONE], [])
    iota(V("pid", 0, 2), [[0, 2]], 1)
    iota(V("uoi", 0, 16), [[1, 2], [16, 8]], 0)
    iota(row("cm"), [[0, 24], [1, 16]], 0, True)
    iota(NUM, [[1, C]], 0, True)
    emit("g", lambda: g.affine_select(EYE[3], ONE[3], [[-1, 516]], A.is_equal, 0.0, 3, 4), [EYE], [ONE])
    iota(V("q16", 0, 24), [[16, 24]], 0)
    ts(V("pmi", 0, 2), V("pid", 0, 2), 15, A.bitwise_and)
    copy(V("uo", 0, 16), V("uoi", 0, 16))
    copy(V("pm", 0, 2), V("pmi", 0, 2))
    ts(CP, PM, 15.0, A.is_lt, HOLD, A.mult)
    ts(row("xd"), row("cm"), PM, A.subtract)
    P, FU, INV, PKU = V("p0", 0, 24), V("f0", 0, 24), V("iu", 0, 24), V("pku", 0, 24)
    ts(row("d1"), row("xd"), 0.0, A.is_equal, -30000.0, A.mult)
    ts(row("d2"), row("xd"), 1.0, A.is_equal, HOLD, A.mult)
    copy(P, V("ppi", 0, 24))
    copy(V("ku", 0, 72), V("pri", 0, 72))
    copy(FU, V("rfi", 0, 24))
    iv = ind(row("iv0"), P)
    emit("v", lambda: g.vector.tensor_copy(iv[3], NUM[3]), [row("iv0")], [NUM, P])
    quant(V("uq", 0, 128), V("up", 0, 128), V("uin", 0, 512))
    UO = V("uo", 0, 16)

    def candidates(t, P, FU, part):
        K = V("ku", 24 * t, 24 * t + 24)
        if part == 0:
            act(row("prow"), ind(NUM, P))
        if part == 1:
            act(row("pk"), ind(row("prow"), K), bias=-MID)

    def differences(t):
        D, B = "dd%d" % t, "ba%d" % t
        if t:
            scan(row("scp"), row("pk"))
            ts(PKU, held("scp"), CP, A.subtract, MID, A.add)
        scan(row("scf"), row("fk"))
        ts(V("pkw", 0, 24), held("scp"), CP, A.subtract, MID, A.add)
        ts(V("pkw", 24, 48), held("scf"), CP, A.subtract, MID, A.add)
        tt(V(D, 24, 72), V("pkw", 0, 48), V(B, 24, 72), A.subtract)
        ts(V(B, 72, 96), V(B, 48, 72), 0.0, A.add)
        tt(V(D, 72, 96), V(D, 48, 72), V(D, 0, 24), A.subtract)
        ts(V("dcp", 0, 96), V(D, 0, 96), CP, A.mult)
        tt(V("bs", 0, 96), V(B, 0, 96), V("dcp", 0, 96), A.subtract)

    candidates(0, P, FU, 0)
    copy(bits(V("uuq", 0, 256), dt.uint32), ind(bits(V("uq", 0, 128), dt.uint32), UO))
    uup, upw = V("uup", 0, 256), ind(V("up", 0, 128), UO)
    emit("s", lambda: g.scalar.activation(uup[3], upw[3], F.Copy), [uup], [upw])
    candidates(0, P, FU, 1)
    act(row("frow"), ind(NUM, FU))
    quant(V("xq0", 0, C), V("xp0", 0, C), V("xin", 0, 1536))
    tt(row("d0"), row("d1"), row("d2"), A.add)
    ts(QW, V("q16", 0, 24), PM, A.add)
    scan(row("scp"), row("pk"))
    for b in range(4):
        quant(V("eq", 128 * b, 128 * b + 128), V("ep", 128 * b, 128 * b + 128), V("eye", 3 - b, 515 - b))
    copy(V("ba0", 24, 48), V("ppi", 0, 24))
    copy(V("ba0", 48, 72), V("rfi", 0, 24))

    def own(t):
        copy(V("ba%d" % t, 0, 24), QW)
        tt(V("dd%d" % t, 0, 24), V("pri", 24 * t, 24 * t + 24), QW, A.subtract)

    for t in range(3):
        last = t == 2
        other = T.cores[rank ^ STEP[t]]
        eng = topo.engines(core, other)
        mask = sum(1 << e for e in eng)
        rid, pnc = topo.addr(other)[:2]
        X, XP = V("xq%d" % t, 0, C), V("xp%d" % t, 0, C)

        def send(dst, src, s, made):
            recs = [e[3] for nm, a, b in flat([made]) for e in acc[nm] if e[2] and e[0] < b and a < e[1]]
            await_("g", recs)
            g.remote_dma(dst[3], src[3], T.sem[s], T.sem.sent, pnc, rid, mask)
            count["sent"] = count.get("sent", 0) + len(eng)
            count[s] = len(eng)
            acc.setdefault(dst[0], []).append((dst[1], dst[2], True, (s, len(eng), {s: len(eng)})))

        mm(4, V("uuq", 0, 128), V("uup", 0, 128), X, XP, C)
        mm(5, V("uuq", 128, 256), V("uup", 128, 256), X, XP, C)
        for b in range(4):
            mm(b, V("eq", 128 * b, 128 * b + 128), V("ep", 128 * b, 128 * b + 128), X, XP, C)
        if t:
            differences(t)
        else:
            ts(PKU, held("scp"), CP, A.subtract, MID, A.add)
            own(0)
        act(row("aw"), V("ps", 2048, 2048 + C), F.Sign, bias=-2.0 ** -93)
        pu, ku = V(P[0], P[1], P[1] + 12), V("pku", 0, 12)
        pv, kv = V(P[0], P[1] + 12, P[2]), V("pku", 12, 24)
        act(V("ar", 0, H), ind(row("aw"), pu), F.Copy)
        act(V("ar", H, C), ind(row("aw"), pv), F.Copy)
        tt(V("er", 0, H), ind(row("aw"), ku), V("ar", 0, H), A.is_equal)
        tt(V("er", H, C), ind(row("aw"), kv), V("ar", H, C), A.is_equal)
        if t == 0:
            act(row("fk"), ind(row("frow"), V("ku", 0, 24)), bias=-MID)
            differences(0)
        act(row("bw"), V("ps", 2560, 2560 + C), F.Sign)
        for b in range(2):
            act(V("fb", C * b, C * b + C), V("ps", 512 * b, 512 * b + C), F.Copy)
        scan(row("sc"), row("er"))
        for i in range(4):
            tt(V("mu", 24 * i, 24 * i + 24), held("sc"), V("dd%d" % t, 24 * i, 24 * i + 24), A.mult)
        tt(V("sel", 0, 72), V("mu", 0, 72), V("bs", 0, 72), A.add)
        tt(V("sel", 72, 96), V("mu", 72, 96), V("bs", 72, 96), A.add)
        copy(V("tu", 0, 72), V("sel", 0, 72))
        TU, P, CU = V("tu", 0, 24), V("tu", 24, 48), V("tu", 48, 72)
        act(row("br"), ind(row("bw"), P), F.Relu)
        for b in (2, 3):
            act(V("fb", C * b, C * b + C), V("ps", 512 * b, 512 * b + C), F.Copy)
        for b in range(3):
            act(V("gb", C * b, C * b + C), ind(V("fb", C * b, C * b + C), P), F.Copy, scale=0.5)
        act(V("gb", 3 * C + H, 4 * C), ind(V("fb", 3 * C, 4 * C), V("tu", 36, 48)), F.Copy, scale=0.5)
        ts(V("ni", 0, 24), V("sel", 72, 96), -191.5, A.add, 1.0 / C, A.mult)
        copy(row("tr"), ind(NUM, TU))
        ts(V("nf", 0, 24), V("ni", 0, 24), -float(C), A.mult)
        tt(row("rr"), ind(row("tr"), CU), row("br"), A.mult)
        tt(V("al", 0, 24), V("sel", 72, 96), V("nf", 0, 24), A.add)
        scan(row("scb"), row("br"))
        ts(V("alc", 0, 24), V("al", 0, 24), CP, A.add)
        ts(V("mm", 0, 24), held("scb"), CP, A.subtract, 0.5, A.is_lt)
        scan(row("sc2"), row("rr"))
        tt(V("ma", 0, 24), V("mm", 0, 24), V("alc", 0, 24), A.mult)
        if not last:
            copy(V("ba%d" % (t + 1), 24, 48), V("sel", 24, 48))
        tt(V("mx", 0, 24), V("ma", 0, 24), held("sc2"), A.max)
        FU = V("fu%d" % t, 0, 24)
        ts(FU, V("mx", 0, 24), CP, A.subtract)
        if t == 0:
            scan(row("sc3"), row("iv0"))
            ts(INV, held("sc3"), CP, A.subtract)
            own(1)
            own(2)
        send(V("lf%d" % t, 0, 24), FU, "af%d" % t, FU)

        def twin(b, h):
            copy(V("gc", C * b + H * h, C * b + H * h + H), V("gb", C * b + H * h, C * b + H * h + H))

        def mix(b, h):
            o = lane("zt", b, H * h, H * h + H)
            tt(o, ind(V("gb", C * b, C * b + C), V(FU[0], 12 * h, 12 * h + 12)), V("gc", C * b + H * h, C * b + H * h + H), A.add)
        ts(V("gb", 3 * C, 3 * C + H), ind(V("fb", 3 * C, 4 * C), V("tu", 24, 36)), 0.5, A.mult)
        twin(0, 1)
        twin(1, 1)
        mix(0, 1)
        mix(1, 1)
        twin(2, 1)
        mix(2, 1)
        twin(3, 1)
        mix(3, 1)
        UQ, UP = V("zuq%d" % t, 0, H), V("zup%d" % t, 0, H)
        quant(UQ, UP, V("zt", 768, 1536))
        send(bits(V("lq%d" % t, 0, H)), bits(UQ), "aq%d" % t, UQ)
        send(V("lp%d" % t, 0, H), UP, "ap%d" % t, UP)
        act(row("ir"), ind(row("tr"), INV), bias=-MID)
        scan(row("sc3"), row("ir"))
        twin(0, 0)
        ts(INV, held("sc3"), CP, A.subtract, MID, A.add)
        if t == 0:
            act(row("prow"), ind(NUM, P))
            act(row("frow"), ind(NUM, FU))
            act(row("hr"), ind(row("frow"), INV), bias=-MID)
            candidates(1, P, FU, 1)
            act(row("fs"), ind(NUM, V("lf0", 0, 24)))
        else:
            act(row("prow"), ind(NUM, P))
            act(row("fs"), ind(NUM, V("lf%d" % t, 0, 24)))
            act(row("ef"), ind(row("fs"), FU))
            act(row("ej"), ind(row("ef"), INV), bias=-MID)
            if not last:
                candidates(t + 1, P, FU, 1)
            else:
                act(row("frow"), ind(NUM, FU))
        for b in (1, 2, 3):
            twin(b, 0)
        for b in range(4):
            mix(b, 0)
            if t == 0 and b == 1:
                scan(row("sc5"), row("hr"))
                ts(V("hu", 0, 24), held("sc5"), CP, A.subtract, MID, A.add)
                act(row("ej"), ind(row("fs"), V("hu", 0, 24)), bias=-MID)
        quant(V("zlq", 0, H), V("zlp", 0, H), V("zt", 0, 768))
        low, up = (0, 1, 2, 5), (4, 6, 7, 0)

        def layer(b, h):
            x = (V("lq%d" % t, 0, H), V("lp%d" % t, 0, H)) if h else (V("zlq", 0, H), V("zlp", 0, H))
            mm((low, up)[h][b], V("wq", 128 * b, 128 * b + 128), V("wp", 128 * b, 128 * b + 128), x[0], x[1], H)

        def cast(b, h):
            o, i = V("bb", C * b + H * h, C * b + H * h + H), 512 * (low, up)[h][b]
            if b == 0:
                ts(o, V("ps", i, i + H), 0.03125, A.mult)
            else:
                act(o, V("ps", i, i + H), F.Copy, scale=0.03125)
        layer(0, 0)
        layer(1, 0)
        layer(0, 1)
        layer(1, 1)
        if t:
            scan(row("sc4"), row("ej"))
        cast(0, 0)
        cast(1, 0)
        if not t:
            scan(row("sc4"), row("ej"))
        ts(V("eu", 0, 24), held("sc4"), CP, A.subtract, MID, A.add)
        if not last:
            ts(V("ba%d" % (t + 1), 48, 72), V("mx", 0, 24), CP, A.subtract)
        cast(0, 1)
        cast(1, 1)
        for b in (2, 3):
            for h in (0, 1):
                layer(b, h)
                cast(b, h)

        def state(b, h=None):
            lo, hi = (0, C) if h is None else (H * h, H * h + H)
            tt(lane("xt", b, lo, hi), ind(V("bb", C * b, C * b + C), V("eu", lo // 16, hi // 16)), V("fb", C * b + lo, C * b + hi), A.add)
        if not last:
            act(row("b3"), ind(V("bb", 3 * C, 4 * C), V("eu", 0, 24)), F.Copy)
            for b in range(3):
                state(b)
            tt(lane("xt", 3, 0, C), row("b3"), V("ps", 1536, 1536 + C), A.add)
            if t:
                act(row("frow"), ind(NUM, FU))
            act(row("fk"), ind(row("frow"), V("ku", 24 * t + 24, 24 * t + 48)), bias=-MID)
            quant(V("xq%d" % (t + 1), 0, C), V("xp%d" % (t + 1), 0, C), V("xt", 0, 1536))
    store(T.pf[:, 0:C], ("prow", 0, C, T.prow[0:128:16, :]))
    store(T.pf[:, C:2 * C], ("frow", 0, C, T.frow[0:128:16, :]))
    quant(V("vq", 0, 128), V("vp", 0, 128), V("vin", 0, 512))
    for b, h in ((0, 0), (0, 1), (1, 0), (1, 1), (2, 0), (3, 0)):
        state(b, h)

    def finish(h):
        X, XP = V("xq3", H * h, H * h + H), V("xp3", H * h, H * h + H)
        quant(X, XP, V("xt", 768 * h, 768 * h + 768))
        mm(4 + h, V("vq", 0, 128), V("vp", 0, 128), X, XP, H)
        store(T.oc[:, 768 * h:768 * h + 768], bits(X))
    finish(0)
    act(V("yo", 0, H), V("ps", 2048, 2048 + H), F.Copy)
    store(T.y[:, 0:H], V("yo", 0, H), "s")
    state(2, 1)
    state(3, 1)
    finish(1)
    for k in range(4):
        store(T.osc[4 * k:4 * k + 4, :], ("xp3", 0, C, T.xp3[32 * k:32 * k + 4, :]), "y" if k % 2 else "s")
    ts(V("yo", H, C), V("ps", 2560, 2560 + H), 1.0, A.mult)
    store(T.y[:, H:C], V("yo", H, C))
    for s in count:
        if know["g"].get(s, 0) < count[s]:
            g.wait_ge(T.sem[s], count[s])
